import numpy as np
import ml_dtypes


def mxq(x, axis, fmt="e4m3"):
    dtype, down = {"e4m3": (ml_dtypes.float8_e4m3fn, 7), "e5m2": (ml_dtypes.float8_e5m2, 14)}[fmt]
    v = np.moveaxis(np.asarray(x, np.float32).astype(ml_dtypes.bfloat16).astype(np.float64), axis, -1)
    blocks = v.reshape(v.shape[:-1] + (-1, 32))
    amax = np.abs(blocks).max(-1, keepdims=True)
    byte = np.maximum(np.where(amax > 0, np.frexp(amax)[1] - 1 + 127, 0) - down, 1)
    scale = np.exp2(byte - 127.0)
    codes = (blocks / scale).astype(np.float32).astype(dtype).astype(np.float64)
    return np.moveaxis((codes * scale).reshape(v.shape), -1, axis)


WIDE = False


def mx_kscale(k):
    if not WIDE:
        return np.ones(k)
    levels = np.array([10, -10, 5, -5, 0])
    if k % 512:
        return np.exp2(np.random.permutation(np.resize(levels, k // 32))).repeat(32)
    a = np.empty((k // 512, 16))
    for p in range(k // 512):
        a[p, :8] = np.random.permutation(np.resize(levels, 8))
        for g in range(8):
            far = levels[np.abs(levels - a[p, g]) >= 10]
            a[p, g + 8] = far[np.random.randint(len(far))]
    return np.exp2(a.ravel()).repeat(32)


BF16 = ml_dtypes.bfloat16


def bf(x):
    return np.asarray(x, np.float32).astype(BF16)


def f64(x):
    return np.asarray(x).astype(np.float64)


E2M1 = np.array([0.0, 0.5, 1.0, 1.5, 2.0, 3.0, 4.0, 6.0, -0.0, -0.5, -1.0, -1.5, -2.0, -3.0, -4.0, -6.0])


def pack_weight(w, fmt):
    k, n = w.shape
    w = f64(bf(w)).reshape(k // 32, 32, n)
    amax = np.abs(w).max(1)
    if fmt == "e4m3":
        byte = np.frexp(amax)[1] - 1 + 127 - 7
    else:
        mant, ex = np.frexp(amax / 6.0)
        byte = np.where(mant > 0.5, ex, ex - 1) + 127
    byte = np.clip(np.where(amax > 0, byte, 1), 1, 254)
    scaled = (w * np.exp2(127.0 - byte)[:, None, :]).reshape(k, n).astype(np.float32)
    by_word = np.ascontiguousarray(scaled.reshape(k // 512, 128, 4, n).transpose(0, 1, 3, 2))
    if fmt == "e4m3":
        words = by_word.astype(ml_dtypes.float8_e4m3fn).view(np.uint8)
    else:
        c = by_word.astype(ml_dtypes.float4_e2m1fn).view(np.uint8) & 0xF
        words = c[..., 0::2] | (c[..., 1::2] << 4)
    return np.ascontiguousarray(words), np.ascontiguousarray(byte.astype(np.uint8).reshape(k // 512, 16, n))


def unpack_weight(words, scales, fmt):
    g, p, n, _ = words.shape
    if fmt == "e4m3":
        vals = np.ascontiguousarray(words).view(ml_dtypes.float8_e4m3fn).astype(np.float64)
    else:
        nib = np.empty((g, p, n, 4), np.uint8)
        nib[..., 0::2] = words & 0xF
        nib[..., 1::2] = words >> 4
        vals = E2M1[nib]
    vals = vals * np.repeat(np.exp2(scales.astype(np.float64) - 127.0), 8, axis=1)[..., None]
    return vals.transpose(0, 1, 3, 2).reshape(g * 512, n)
def pack4(w):
    words, scales = pack_weight(w, "e2m1")
    return words.reshape(words.shape[0], 128, -1), scales


def unpack4(words, scales):
    return unpack_weight(words.reshape(words.shape[0], 128, -1, 2), scales, "e2m1")


B, D, H = 512, 1024, 2048


def setup_inputs():
    s, t = mx_kscale(D), mx_kscale(H)
    x = np.random.standard_normal((B, D)) * s
    rates = np.tanh(np.random.standard_normal((B, H))) * t
    wx = np.random.standard_normal((D, H)) / np.sqrt(D) / s[:, None]
    wh = np.random.standard_normal((H, H)) / np.sqrt(H) / t[:, None]
    wx_words, wx_scales = pack_weight(wx, "e4m3")
    wh_words, wh_scales = pack4(wh)
    return {"x": bf(x),
            "rates": bf(rates),
            "u": bf(np.random.standard_normal((B, H))),
            "wx_words": wx_words, "wx_scales": wx_scales,
            "wh_words": wh_words, "wh_scales": wh_scales,
            "leak": bf(np.random.uniform(0.5, 0.95, H)),
            "bias": bf(0.3 * np.random.standard_normal(H))}


def reference(x, rates, u, wx_words, wx_scales, wh_words, wh_scales, leak, bias):
    drive = mxq(f64(x), 1, "e4m3") @ unpack_weight(wx_words, wx_scales, "e4m3")
    recur = mxq(f64(rates), 1, "e4m3") @ unpack4(wh_words, wh_scales)
    u_new = (drive + recur) + f64(leak) * f64(u) + f64(bias)
    r_new = np.tanh(u_new)
    return u_new, r_new

@@ -1,0 +1,222 @@
+from contextlib import ExitStack
+
+import concourse.mybir as mybir
+from concourse.masks import make_identity
+
+B, D, H = 512, 1024, 2048
+FLOPS = 2 * B * (D + H) * H
+
+F32 = mybir.dt.float32
+BF16 = mybir.dt.bfloat16
+I32 = mybir.dt.int32
+U32 = mybir.dt.uint32
+U8 = mybir.dt.uint8
+FP8X4 = mybir.dt.float8_e4m3fn_x4
+FP4X4 = mybir.dt.float4_e2m1fn_x4
+ADD = mybir.AluOpType.add
+MULT = mybir.AluOpType.mult
+TANH = mybir.ActivationFunctionType.Tanh
+
+P = 128
+N_TILE = 512
+HALF = H // 2
+X_PASSES = D // 512
+H_PASSES = H // 512
+PASSES = X_PASSES + H_PASSES
+WORK_BANKS = 6
+
+
+def tile_leaky_recurrent_step_s1_kernel(
+    tc, x, rates, u, wx_words, wx_scales, wh_words, wh_scales, leak, bias, out_0, out_1
+):
+    nc = tc.nc
+    with ExitStack() as ctx:
+        keep = ctx.enter_context(tc.tile_pool(name="keep", bufs=1))
+        stage = ctx.enter_context(tc.tile_pool(name="stage", bufs=4))
+        psum = ctx.enter_context(tc.psum_pool(name="psum", bufs=1))
+        ctx.enter_context(tc.manual_schedule())
+
+        bank_uses = []
+
+        def next_bank():
+            n = len(bank_uses)
+            bank_uses.append(n)
+            return psum.tile([P, N_TILE], F32, name="work%d" % n, tag="work%d" % (n % WORK_BANKS))
+
+        def pair_rows(t, h):
+            return t[256 * h : 256 * (h + 1), :].rearrange("(p j) n -> p j n", j=2)
+
+        def load_pair(t, h, name):
+            sb = keep.tile([P, 2 * t.shape[1]], BF16, name="%s%d" % (name, h), align_bytes=64)
+            nc.sync.dma_start(out=sb[:], in_=pair_rows(t, h).rearrange("p j n -> p (j n)"))
+            return sb
+
+        leak_col = keep.tile([P, 2, 8], BF16, align_bytes=64)
+        bias_col = keep.tile([P, 2, 8], BF16, align_bytes=64)
+        nc.scalar.dma_start(out=leak_col[:], in_=leak.rearrange("(a n i) -> n a i", a=2, i=8))
+        nc.scalar.dma_start(out=bias_col[:], in_=bias.rearrange("(a n i) -> n a i", a=2, i=8))
+
+        ident = keep.tile([P, P], F32, align_bytes=64)
+        make_identity(nc, ident[:])
+
+        wx_plane = keep.tile([P, X_PASSES, H], U8, align_bytes=64)
+        wh_plane = keep.tile([P, H_PASSES, H], U8, align_bytes=64)
+        nc.vector.memset(wx_plane[:].bitcast(I32), 0)
+        nc.vector.memset(wh_plane[:].bitcast(I32), 0)
+
+        x_sb, rates_sb, u_sb = {}, {}, {}
+        for h in range(2):
+            rates_sb[h] = load_pair(rates, h, "rates")
+            x_sb[h] = load_pair(x, h, "x")
+        for plane, scales in ((wx_plane, wx_scales), (wh_plane, wh_scales)):
+            for r in range(4):
+                nc.sync.dma_start(
+                    out=plane[r:P:32, :, :].bitcast(I32),
+                    in_=scales.rearrange("g q n -> q g n")[r:16:4, :, :].bitcast(I32),
+                )
+
+        wx_rows = wx_words.rearrange("g p n t -> p g (n t)")
+        wh_rows = wh_words.rearrange("g p n -> p g n")
+        weights = {}
+
+        def load_weights(rows, first_pass, g0, g1, a, col_bytes):
+            width = HALF * col_bytes
+            sb = keep.tile([P, g1 - g0, width], U8, name="w%d_%d" % (first_pass + g0, a), align_bytes=64)
+            nc.sync.dma_start(
+                out=sb[:].bitcast(I32), in_=rows[:, g0:g1, a * width : (a + 1) * width].bitcast(I32)
+            )
+            for g in range(g0, g1):
+                weights[(first_pass + g, a)] = sb[:, g - g0, :]
+
+        load_weights(wx_rows, 0, 0, 1, 0, 4)
+        load_weights(wx_rows, 0, 1, 2, 0, 4)
+        load_weights(wh_rows, X_PASSES, 0, 2, 0, 2)
+        load_weights(wh_rows, X_PASSES, 2, 4, 0, 2)
+        for h in range(2):
+            u_sb[h] = load_pair(u, h, "u")
+        load_weights(wx_rows, 0, 0, 2, 1, 4)
+        load_weights(wh_rows, X_PASSES, 0, 4, 1, 2)
+
+        def spread(bank, col, a):
+            words = col[:].bitcast(F32)
+            for j in range(4):
+                nc.tensor.transpose(
+                    bank[:, j:N_TILE:4], words[:, a, j : j + 1].to_broadcast([P, P]), ident[:]
+                )
+
+        leak_all = keep.tile([P, H], BF16, align_bytes=64)
+        bias_bank = {}
+        for a in range(2):
+            bank = next_bank()
+            spread(bank, leak_col, a)
+            nc.scalar.copy(out=leak_all[:, a * HALF : (a + 1) * HALF].bitcast(F32), in_=bank[:])
+        for a in range(2):
+            bias_bank[a] = psum.tile([P, N_TILE], F32, name="bias%d" % a, tag="bias%d" % a)
+            spread(bias_bank[a], bias_col, a)
+
+        codes, planes = {}, {}
+
+        def turn(src, h, g, on_vector):
+            words = src[:].bitcast(F32)
+            row_words = words.shape[1] // 2
+            bank = next_bank()
+            for j in range(2):
+                for e in range(2):
+                    first = j * row_words + 256 * g
+                    slot = 2 * j + e
+                    nc.tensor.transpose(
+                        bank[:, slot * P : (slot + 1) * P], words[:, first + e : first + 256 : 2], ident[:]
+                    )
+            grouped = stage.tile([P, 2 * P * 4], BF16, tag="grouped", align_bytes=64)
+            dst = grouped[:].bitcast(F32).rearrange("p (j b e) -> p j b e", j=2, e=2)
+            turned = bank[:].rearrange("p (j e b) -> p j b e", j=2, e=2)
+            if on_vector:
+                nc.vector.tensor_copy(out=dst, in_=turned)
+            else:
+                nc.scalar.copy(out=dst, in_=turned)
+            return grouped
+
+        def quantize(grouped, h, k_pass):
+            codes[(h, k_pass)] = keep.tile([P, 2 * P], U32, name="codes%d_%d" % (h, k_pass), align_bytes=64)
+            planes[(h, k_pass)] = keep.tile([P, 2 * P], U8, name="plane%d_%d" % (h, k_pass), align_bytes=64)
+            nc.vector.quantize_mx(
+                out=codes[(h, k_pass)][:].bitcast(FP8X4), scales=planes[(h, k_pass)][:], in_=grouped[:]
+            )
+
+        steps = []
+        for h in range(2):
+            steps.extend((rates_sb[h], h, g, X_PASSES + g) for g in range(H_PASSES))
+            steps.extend((x_sb[h], h, g, g) for g in range(X_PASSES))
+        pending = None
+        for i, (src, h, g, k_pass) in enumerate(steps):
+            grouped = turn(src, h, g, i % 3 == 2)
+            if pending is not None:
+                quantize(*pending)
+            pending = (grouped, h, k_pass)
+        quantize(*pending)
+
+        tiles = [(h, j, a, c) for a in range(2) for h in range(2) for j in range(2) for c in range(2)]
+        acc, base, u_new, r_new = {}, {}, {}, {}
+
+        def mx_pass(i, k_pass):
+            h, j, a, c = tiles[i]
+            if k_pass == 0:
+                acc[i] = next_bank()
+            col0 = a * HALF + c * N_TILE
+            if k_pass < X_PASSES:
+                rhs = weights[(k_pass, a)][:, c * N_TILE * 4 : (c + 1) * N_TILE * 4].bitcast(FP8X4)
+                rhs_scale = wx_plane[:, k_pass, col0 : col0 + N_TILE]
+            else:
+                rhs = weights[(k_pass, a)][:, c * N_TILE * 2 : (c + 1) * N_TILE * 2].bitcast(FP4X4)
+                rhs_scale = wh_plane[:, k_pass - X_PASSES, col0 : col0 + N_TILE]
+            nc.tensor.matmul_mx(
+                out=acc[i][:],
+                lhsT=codes[(h, k_pass)][:, j * P : (j + 1) * P].bitcast(FP8X4),
+                lhsT_scale=planes[(h, k_pass)][:, j * P : (j + 1) * P],
+                rhs=rhs,
+                rhs_scale=rhs_scale,
+                start=(k_pass == 0),
+                stop=(k_pass == PASSES - 1),
+            )
+
+        def make_base(i):
+            h, j, a, c = tiles[i]
+            col0 = a * HALF + c * N_TILE
+            base[i] = stage.tile([P, N_TILE], F32, name="base%d" % i, tag="base", bufs=6)
+            nc.gpsimd.tensor_tensor(
+                out=base[i][:],
+                in0=u_sb[h][:, j * H + col0 : j * H + col0 + N_TILE],
+                in1=leak_all[:, col0 : col0 + N_TILE],
+                op=MULT,
+            )
+            nc.vector.tensor_tensor(
+                out=base[i][:],
+                in0=base[i][:],
+                in1=bias_bank[a][:].bitcast(BF16)[:, c * N_TILE : (c + 1) * N_TILE],
+                op=ADD,
+            )
+
+        def finish(i):
+            h, j, a, c = tiles[i]
+            if c == 0:
+                u_new[(h, j, a)] = keep.tile([P, HALF], F32, name="u_new%d" % i)
+                r_new[(h, j, a)] = keep.tile([P, HALF], F32, name="r_new%d" % i)
+            cols = slice(c * N_TILE, (c + 1) * N_TILE)
+            nc.vector.tensor_tensor(out=u_new[(h, j, a)][:, cols], in0=acc[i][:], in1=base[i][:], op=ADD)
+            nc.scalar.activation(out=r_new[(h, j, a)][:, cols], in_=u_new[(h, j, a)][:, cols], func=TANH)
+            if c == 1:
+                half_cols = slice(a * HALF, (a + 1) * HALF)
+                nc.sync.dma_start(out=pair_rows(out_0, h)[:, j, half_cols], in_=u_new[(h, j, a)][:])
+                nc.sync.dma_start(out=pair_rows(out_1, h)[:, j, half_cols], in_=r_new[(h, j, a)][:])
+
+        first_wave = 4
+        for k_pass in range(4):
+            for i in range(first_wave):
+                mx_pass(i, k_pass)
+        make_base(0)
+        for i in range(len(tiles)):
+            for k_pass in range(4 if i < first_wave else 0, PASSES):
+                mx_pass(i, k_pass)
+            if i + 1 < len(tiles):
+                make_base(i + 1)
+            finish(i)

@@ -59,21 +59,26 @@ def tile_leaky_recurrent_step_s1_kernel(
         ident = keep.tile([P, P], F32, align_bytes=64)
         make_identity(nc, ident[:])
 
-        wx_plane = keep.tile([P, X_PASSES, H], U8, align_bytes=64)
+        wx_plane = keep.tile([P, H], U8, align_bytes=64)
         wh_plane = keep.tile([P, H_PASSES, H], U8, align_bytes=64)
         nc.vector.memset(wx_plane[:].bitcast(I32), 0)
         nc.vector.memset(wh_plane[:].bitcast(I32), 0)
+
+        for q in range(4):
+            nc.gpsimd.dma_start(
+                out=wx_plane[32 * q + 4 : 32 * q + 12, :].bitcast(I32),
+                in_=wx_scales[:, 4 * q : 4 * q + 4, :].bitcast(I32),
+            )
+        for r in range(4):
+            nc.gpsimd.dma_start(
+                out=wh_plane[r:P:32, :, :].bitcast(I32),
+                in_=wh_scales.rearrange("g q n -> q g n")[r:16:4, :, :].bitcast(I32),
+            )
 
         x_sb, rates_sb, u_sb = {}, {}, {}
         for h in range(2):
             rates_sb[h] = load_pair(rates, h, "rates")
             x_sb[h] = load_pair(x, h, "x")
-        for plane, scales in ((wx_plane, wx_scales), (wh_plane, wh_scales)):
-            for r in range(4):
-                nc.sync.dma_start(
-                    out=plane[r:P:32, :, :].bitcast(I32),
-                    in_=scales.rearrange("g q n -> q g n")[r:16:4, :, :].bitcast(I32),
-                )
 
         wx_rows = wx_words.rearrange("g p n t -> p g (n t)")
         wh_rows = wh_words.rearrange("g p n -> p g n")
@@ -101,18 +106,23 @@ def tile_leaky_recurrent_step_s1_kernel(
             words = col[:].bitcast(F32)
             for j in range(4):
                 nc.tensor.transpose(
-                    bank[:, j:N_TILE:4], words[:, a, j : j + 1].to_broadcast([P, P]), ident[:]
+                    bank[:, j * P : (j + 1) * P], words[:, a, j : j + 1].to_broadcast([P, P]), ident[:]
                 )
 
         leak_all = keep.tile([P, H], BF16, align_bytes=64)
         bias_bank = {}
-        for a in range(2):
+
+        def spread_half(a):
             bank = next_bank()
             spread(bank, leak_col, a)
-            nc.scalar.copy(out=leak_all[:, a * HALF : (a + 1) * HALF].bitcast(F32), in_=bank[:])
-        for a in range(2):
+            nc.scalar.copy(
+                out=leak_all[:, a * HALF : (a + 1) * HALF].bitcast(F32).rearrange("p (n j) -> p n j", j=4),
+                in_=bank[:].rearrange("p (j n) -> p n j", j=4),
+            )
             bias_bank[a] = psum.tile([P, N_TILE], F32, name="bias%d" % a, tag="bias%d" % a)
             spread(bias_bank[a], bias_col, a)
+
+        spread_half(0)
 
         codes, planes = {}, {}
 
@@ -165,7 +175,7 @@ def tile_leaky_recurrent_step_s1_kernel(
             col0 = a * HALF + c * N_TILE
             if k_pass < X_PASSES:
                 rhs = weights[(k_pass, a)][:, c * N_TILE * 4 : (c + 1) * N_TILE * 4].bitcast(FP8X4)
-                rhs_scale = wx_plane[:, k_pass, col0 : col0 + N_TILE]
+                rhs_scale = wx_plane[4 * (k_pass + 1) : P, col0 : col0 + N_TILE]
             else:
                 rhs = weights[(k_pass, a)][:, c * N_TILE * 2 : (c + 1) * N_TILE * 2].bitcast(FP4X4)
                 rhs_scale = wh_plane[:, k_pass - X_PASSES, col0 : col0 + N_TILE]
@@ -190,9 +200,11 @@ def tile_leaky_recurrent_step_s1_kernel(
                 op=MULT,
             )
             nc.vector.tensor_tensor(
-                out=base[i][:],
-                in0=base[i][:],
-                in1=bias_bank[a][:].bitcast(BF16)[:, c * N_TILE : (c + 1) * N_TILE],
+                out=base[i][:].rearrange("p (n j e) -> p n j e", j=4, e=2),
+                in0=base[i][:].rearrange("p (n j e) -> p n j e", j=4, e=2),
+                in1=bias_bank[a][:].bitcast(BF16).rearrange("p (j n e) -> p n j e", j=4, e=2)[
+                    :, c * 64 : (c + 1) * 64, :, :
+                ],
                 op=ADD,
             )
 
@@ -204,7 +216,11 @@ def tile_leaky_recurrent_step_s1_kernel(
             cols = slice(c * N_TILE, (c + 1) * N_TILE)
             nc.vector.tensor_tensor(out=u_new[(h, j, a)][:, cols], in0=acc[i][:], in1=base[i][:], op=ADD)
             nc.scalar.activation(out=r_new[(h, j, a)][:, cols], in_=u_new[(h, j, a)][:, cols], func=TANH)
-            if c == 1:
+            if i >= len(tiles) - 2:
+                out_cols = slice(a * HALF + c * N_TILE, a * HALF + (c + 1) * N_TILE)
+                nc.sync.dma_start(out=pair_rows(out_0, h)[:, j, out_cols], in_=u_new[(h, j, a)][:, cols])
+                nc.sync.dma_start(out=pair_rows(out_1, h)[:, j, out_cols], in_=r_new[(h, j, a)][:, cols])
+            elif c == 1:
                 half_cols = slice(a * HALF, (a + 1) * HALF)
                 nc.sync.dma_start(out=pair_rows(out_0, h)[:, j, half_cols], in_=u_new[(h, j, a)][:])
                 nc.sync.dma_start(out=pair_rows(out_1, h)[:, j, half_cols], in_=r_new[(h, j, a)][:])
@@ -220,3 +236,5 @@ def tile_leaky_recurrent_step_s1_kernel(
             if i + 1 < len(tiles):
                 make_base(i + 1)
             finish(i)
+            if i == 5:
+                spread_half(1)

@@ -51,34 +51,42 @@ def tile_leaky_recurrent_step_s1_kernel(
             nc.sync.dma_start(out=sb[:], in_=pair_rows(t, h).rearrange("p j n -> p (j n)"))
             return sb
 
-        leak_col = keep.tile([P, 2, 8], BF16, align_bytes=64)
-        bias_col = keep.tile([P, 2, 8], BF16, align_bytes=64)
-        nc.scalar.dma_start(out=leak_col[:], in_=leak.rearrange("(a n i) -> n a i", a=2, i=8))
-        nc.scalar.dma_start(out=bias_col[:], in_=bias.rearrange("(a n i) -> n a i", a=2, i=8))
+        vec_rows = keep.tile([P, 2 * P], BF16, align_bytes=64)
+        nc.gpsimd.memset(vec_rows[:].bitcast(F32), 0.0)
+        nc.sync.dma_start(out=vec_rows[0:8, :], in_=leak.rearrange("(r n) -> r n", r=8))
+        nc.sync.dma_start(out=vec_rows[8:16, :], in_=bias.rearrange("(r n) -> r n", r=8))
 
         ident = keep.tile([P, P], F32, align_bytes=64)
         make_identity(nc, ident[:])
 
-        wx_plane = keep.tile([P, H], U8, align_bytes=64)
-        wh_plane = keep.tile([P, H_PASSES, H], U8, align_bytes=64)
-        nc.vector.memset(wx_plane[:].bitcast(I32), 0)
-        nc.vector.memset(wh_plane[:].bitcast(I32), 0)
+        wx_plane, wh_plane = {}, {}
 
-        for q in range(4):
-            nc.gpsimd.dma_start(
-                out=wx_plane[32 * q + 4 : 32 * q + 12, :].bitcast(I32),
-                in_=wx_scales[:, 4 * q : 4 * q + 4, :].bitcast(I32),
-            )
-        for r in range(4):
-            nc.gpsimd.dma_start(
-                out=wh_plane[r:P:32, :, :].bitcast(I32),
-                in_=wh_scales.rearrange("g q n -> q g n")[r:16:4, :, :].bitcast(I32),
-            )
+        def clear_planes(a):
+            wx_plane[a] = keep.tile([P, HALF], U8, name="wx_plane%d" % a, align_bytes=64)
+            wh_plane[a] = keep.tile([P, H_PASSES, HALF], U8, name="wh_plane%d" % a, align_bytes=64)
+            nc.vector.memset(wx_plane[a][:].bitcast(I32), 0)
+            nc.vector.memset(wh_plane[a][:].bitcast(I32), 0)
+
+        def load_scales(a):
+            cols = slice(a * HALF, (a + 1) * HALF)
+            for q in range(4):
+                nc.sync.dma_start(
+                    out=wx_plane[a][32 * q + 4 : 32 * q + 12, :].bitcast(I32),
+                    in_=wx_scales[:, 4 * q : 4 * q + 4, cols].bitcast(I32),
+                )
+            for r in range(4):
+                nc.sync.dma_start(
+                    out=wh_plane[a][r:P:32, :, :].bitcast(I32),
+                    in_=wh_scales.rearrange("g q n -> q g n")[r:16:4, :, cols].bitcast(I32),
+                )
 
         x_sb, rates_sb, u_sb = {}, {}, {}
         for h in range(2):
             rates_sb[h] = load_pair(rates, h, "rates")
             x_sb[h] = load_pair(x, h, "x")
+        clear_planes(0)
+        clear_planes(1)
+        load_scales(0)
 
         wx_rows = wx_words.rearrange("g p n t -> p g (n t)")
         wh_rows = wh_words.rearrange("g p n -> p g n")
@@ -93,34 +101,44 @@ def tile_leaky_recurrent_step_s1_kernel(
             for g in range(g0, g1):
                 weights[(first_pass + g, a)] = sb[:, g - g0, :]
 
+        def load_u(h, a0, a1):
+            sb = keep.tile([P, 2, (a1 - a0) * HALF], BF16, name="u%d_%d" % (h, a0), align_bytes=64)
+            nc.sync.dma_start(out=sb[:], in_=pair_rows(u, h)[:, :, a0 * HALF : a1 * HALF])
+            for a in range(a0, a1):
+                u_sb[(h, a)] = sb[:, :, (a - a0) * HALF : (a - a0 + 1) * HALF]
+
         load_weights(wx_rows, 0, 0, 1, 0, 4)
         load_weights(wx_rows, 0, 1, 2, 0, 4)
+        load_u(0, 0, 1)
         load_weights(wh_rows, X_PASSES, 0, 2, 0, 2)
         load_weights(wh_rows, X_PASSES, 2, 4, 0, 2)
-        for h in range(2):
-            u_sb[h] = load_pair(u, h, "u")
+        load_u(1, 0, 2)
+        load_scales(1)
         load_weights(wx_rows, 0, 0, 2, 1, 4)
+        load_u(0, 1, 2)
         load_weights(wh_rows, X_PASSES, 0, 4, 1, 2)
 
-        def spread(bank, col, a):
-            words = col[:].bitcast(F32)
+        bank = next_bank()
+        nc.tensor.transpose(bank[:, 0:P], vec_rows[:].bitcast(F32), ident[:])
+        vec_cols = keep.tile([P, 16], F32, align_bytes=64)
+        nc.scalar.copy(out=vec_cols[:], in_=bank[:, 0:16])
+
+        def spread(bank, first_row):
             for j in range(4):
+                row = first_row + j
                 nc.tensor.transpose(
-                    bank[:, j * P : (j + 1) * P], words[:, a, j : j + 1].to_broadcast([P, P]), ident[:]
+                    bank[:, j * P : (j + 1) * P], vec_cols[:, row : row + 1].to_broadcast([P, P]), ident[:]
                 )
 
-        leak_all = keep.tile([P, H], BF16, align_bytes=64)
-        bias_bank = {}
+        leak_all, bias_bank = {}, {}
 
         def spread_half(a):
             bank = next_bank()
-            spread(bank, leak_col, a)
-            nc.scalar.copy(
-                out=leak_all[:, a * HALF : (a + 1) * HALF].bitcast(F32).rearrange("p (n j) -> p n j", j=4),
-                in_=bank[:].rearrange("p (j n) -> p n j", j=4),
-            )
+            spread(bank, 4 * a)
+            leak_all[a] = keep.tile([P, HALF], BF16, name="leak_all%d" % a, align_bytes=64)
+            nc.scalar.copy(out=leak_all[a][:].bitcast(F32), in_=bank[:])
             bias_bank[a] = psum.tile([P, N_TILE], F32, name="bias%d" % a, tag="bias%d" % a)
-            spread(bias_bank[a], bias_col, a)
+            spread(bias_bank[a], 8 + 4 * a)
 
         spread_half(0)
 
@@ -164,6 +182,7 @@ def tile_leaky_recurrent_step_s1_kernel(
                 quantize(*pending)
             pending = (grouped, h, k_pass)
         quantize(*pending)
+        spread_half(1)
 
         tiles = [(h, j, a, c) for a in range(2) for h in range(2) for j in range(2) for c in range(2)]
         acc, base, u_new, r_new = {}, {}, {}, {}
@@ -172,13 +191,13 @@ def tile_leaky_recurrent_step_s1_kernel(
             h, j, a, c = tiles[i]
             if k_pass == 0:
                 acc[i] = next_bank()
-            col0 = a * HALF + c * N_TILE
+            cols = slice(c * N_TILE, (c + 1) * N_TILE)
             if k_pass < X_PASSES:
                 rhs = weights[(k_pass, a)][:, c * N_TILE * 4 : (c + 1) * N_TILE * 4].bitcast(FP8X4)
-                rhs_scale = wx_plane[4 * (k_pass + 1) : P, col0 : col0 + N_TILE]
+                rhs_scale = wx_plane[a][4 * (k_pass + 1) : P, cols]
             else:
                 rhs = weights[(k_pass, a)][:, c * N_TILE * 2 : (c + 1) * N_TILE * 2].bitcast(FP4X4)
-                rhs_scale = wh_plane[:, k_pass - X_PASSES, col0 : col0 + N_TILE]
+                rhs_scale = wh_plane[a][:, k_pass - X_PASSES, cols]
             nc.tensor.matmul_mx(
                 out=acc[i][:],
                 lhsT=codes[(h, k_pass)][:, j * P : (j + 1) * P].bitcast(FP8X4),
@@ -189,23 +208,17 @@ def tile_leaky_recurrent_step_s1_kernel(
                 stop=(k_pass == PASSES - 1),
             )
 
-        def make_base(i):
+        def leak_times_u(i, engine):
             h, j, a, c = tiles[i]
-            col0 = a * HALF + c * N_TILE
-            base[i] = stage.tile([P, N_TILE], F32, name="base%d" % i, tag="base", bufs=6)
-            nc.gpsimd.tensor_tensor(
-                out=base[i][:],
-                in0=u_sb[h][:, j * H + col0 : j * H + col0 + N_TILE],
-                in1=leak_all[:, col0 : col0 + N_TILE],
-                op=MULT,
-            )
+            cols = slice(c * N_TILE, (c + 1) * N_TILE)
+            base[i] = stage.tile([P, N_TILE], F32, name="base%d" % i, tag="base", bufs=8)
+            engine.tensor_tensor(out=base[i][:], in0=u_sb[(h, a)][:, j, cols], in1=leak_all[a][:, cols], op=MULT)
+
+        def add_bias(i):
+            h, j, a, c = tiles[i]
+            cols = slice(c * N_TILE, (c + 1) * N_TILE)
             nc.vector.tensor_tensor(
-                out=base[i][:].rearrange("p (n j e) -> p n j e", j=4, e=2),
-                in0=base[i][:].rearrange("p (n j e) -> p n j e", j=4, e=2),
-                in1=bias_bank[a][:].bitcast(BF16).rearrange("p (j n e) -> p n j e", j=4, e=2)[
-                    :, c * 64 : (c + 1) * 64, :, :
-                ],
-                op=ADD,
+                out=base[i][:], in0=base[i][:], in1=bias_bank[a][:].bitcast(BF16)[:, cols], op=ADD
             )
 
         def finish(i):
@@ -214,7 +227,7 @@ def tile_leaky_recurrent_step_s1_kernel(
                 u_new[(h, j, a)] = keep.tile([P, HALF], F32, name="u_new%d" % i)
                 r_new[(h, j, a)] = keep.tile([P, HALF], F32, name="r_new%d" % i)
             cols = slice(c * N_TILE, (c + 1) * N_TILE)
-            nc.vector.tensor_tensor(out=u_new[(h, j, a)][:, cols], in0=acc[i][:], in1=base[i][:], op=ADD)
+            nc.vector.tensor_tensor(out=u_new[(h, j, a)][:, cols], in0=base[i][:], in1=acc[i][:], op=ADD)
             nc.scalar.activation(out=r_new[(h, j, a)][:, cols], in_=u_new[(h, j, a)][:, cols], func=TANH)
             if i >= len(tiles) - 2:
                 out_cols = slice(a * HALF + c * N_TILE, a * HALF + (c + 1) * N_TILE)
@@ -229,12 +242,14 @@ def tile_leaky_recurrent_step_s1_kernel(
         for k_pass in range(4):
             for i in range(first_wave):
                 mx_pass(i, k_pass)
-        make_base(0)
+        for i in range(first_wave):
+            leak_times_u(i, nc.vector)
+        for i in range(first_wave):
+            add_bias(i)
         for i in range(len(tiles)):
             for k_pass in range(4 if i < first_wave else 0, PASSES):
                 mx_pass(i, k_pass)
-            if i + 1 < len(tiles):
-                make_base(i + 1)
+            if first_wave <= i + 1 < len(tiles):
+                leak_times_u(i + 1, nc.gpsimd)
+                add_bias(i + 1)
             finish(i)
-            if i == 5:
-                spread_half(1)

@@ -23,7 +23,9 @@ HALF = H // 2
 X_PASSES = D // 512
 H_PASSES = H // 512
 PASSES = X_PASSES + H_PASSES
-WORK_BANKS = 6
+SUM_BANKS = (0, 5, 4, 1, 2, 3)
+TURN_BANKS = (4, 5, 6)
+BIAS_BANKS = (7, 6)
 
 
 def tile_leaky_recurrent_step_s1_kernel(
@@ -38,10 +40,15 @@ def tile_leaky_recurrent_step_s1_kernel(
 
         bank_uses = []
 
+        def take_bank(number):
+            bank_uses.append(number)
+            return psum.tile([P, N_TILE], F32, name="bank_use%d" % len(bank_uses), tag="bank%d" % number)
+
+        turn_uses = []
+
         def next_bank():
-            n = len(bank_uses)
-            bank_uses.append(n)
-            return psum.tile([P, N_TILE], F32, name="work%d" % n, tag="work%d" % (n % WORK_BANKS))
+            turn_uses.append(0)
+            return take_bank(TURN_BANKS[len(turn_uses) % len(TURN_BANKS)])
 
         def pair_rows(t, h):
             return t[256 * h : 256 * (h + 1), :].rearrange("(p j) n -> p j n", j=2)
@@ -67,13 +74,16 @@ def tile_leaky_recurrent_step_s1_kernel(
             nc.vector.memset(wx_plane[a][:].bitcast(I32), 0)
             nc.vector.memset(wh_plane[a][:].bitcast(I32), 0)
 
-        def load_scales(a):
+        def load_wx_scales(a):
             cols = slice(a * HALF, (a + 1) * HALF)
             for q in range(4):
                 nc.sync.dma_start(
                     out=wx_plane[a][32 * q + 4 : 32 * q + 12, :].bitcast(I32),
                     in_=wx_scales[:, 4 * q : 4 * q + 4, cols].bitcast(I32),
                 )
+
+        def load_wh_scales(a):
+            cols = slice(a * HALF, (a + 1) * HALF)
             for r in range(4):
                 nc.sync.dma_start(
                     out=wh_plane[a][r:P:32, :, :].bitcast(I32),
@@ -81,12 +91,8 @@ def tile_leaky_recurrent_step_s1_kernel(
                 )
 
         x_sb, rates_sb, u_sb = {}, {}, {}
-        for h in range(2):
-            rates_sb[h] = load_pair(rates, h, "rates")
-            x_sb[h] = load_pair(x, h, "x")
         clear_planes(0)
         clear_planes(1)
-        load_scales(0)
 
         wx_rows = wx_words.rearrange("g p n t -> p g (n t)")
         wh_rows = wh_words.rearrange("g p n -> p g n")
@@ -107,16 +113,23 @@ def tile_leaky_recurrent_step_s1_kernel(
             for a in range(a0, a1):
                 u_sb[(h, a)] = sb[:, :, (a - a0) * HALF : (a - a0 + 1) * HALF]
 
+        x_sb[0] = load_pair(x, 0, "x")
+        load_wx_scales(0)
         load_weights(wx_rows, 0, 0, 1, 0, 4)
         load_weights(wx_rows, 0, 1, 2, 0, 4)
-        load_u(0, 0, 1)
+        rates_sb[0] = load_pair(rates, 0, "rates")
+        load_wh_scales(0)
         load_weights(wh_rows, X_PASSES, 0, 2, 0, 2)
         load_weights(wh_rows, X_PASSES, 2, 4, 0, 2)
+        x_sb[1] = load_pair(x, 1, "x")
+        load_u(0, 0, 1)
+        rates_sb[1] = load_pair(rates, 1, "rates")
         load_u(1, 0, 2)
-        load_scales(1)
+        load_wx_scales(1)
         load_weights(wx_rows, 0, 0, 2, 1, 4)
-        load_u(0, 1, 2)
+        load_wh_scales(1)
         load_weights(wh_rows, X_PASSES, 0, 4, 1, 2)
+        load_u(0, 1, 2)
 
         bank = next_bank()
         nc.tensor.transpose(bank[:, 0:P], vec_rows[:].bitcast(F32), ident[:])
@@ -132,30 +145,33 @@ def tile_leaky_recurrent_step_s1_kernel(
 
         leak_all, bias_bank = {}, {}
 
-        def spread_half(a):
+        def spread_leak(a):
             bank = next_bank()
             spread(bank, 4 * a)
             leak_all[a] = keep.tile([P, HALF], BF16, name="leak_all%d" % a, align_bytes=64)
             nc.scalar.copy(out=leak_all[a][:].bitcast(F32), in_=bank[:])
-            bias_bank[a] = psum.tile([P, N_TILE], F32, name="bias%d" % a, tag="bias%d" % a)
-            spread(bias_bank[a], 8 + 4 * a)
 
-        spread_half(0)
+        def spread_bias(a):
+            bias_bank[a] = take_bank(BIAS_BANKS[a])
+            spread(bias_bank[a], 8 + 4 * a)
 
         codes, planes = {}, {}
 
-        def turn(src, h, g, on_vector):
-            words = src[:].bitcast(F32)
-            row_words = words.shape[1] // 2
+        def sort_words(src, g):
+            words = src[:].bitcast(F32).rearrange("p (j w) -> p j w", j=2)[:, :, 256 * g : 256 * (g + 1)]
+            by_parity = stage.tile([P, 4 * P], F32, tag="by_parity", bufs=8, align_bytes=64)
+            nc.vector.tensor_copy(
+                out=by_parity[:].rearrange("p (j e c i) -> p j c e i", j=2, e=2, i=4),
+                in_=words.rearrange("p j (c i e) -> p j c e i", e=2, i=4),
+            )
+            return by_parity
+
+        def turn(by_parity, on_vector):
             bank = next_bank()
-            for j in range(2):
-                for e in range(2):
-                    first = j * row_words + 256 * g
-                    slot = 2 * j + e
-                    nc.tensor.transpose(
-                        bank[:, slot * P : (slot + 1) * P], words[:, first + e : first + 256 : 2], ident[:]
-                    )
-            grouped = stage.tile([P, 2 * P * 4], BF16, tag="grouped", align_bytes=64)
+            for slot in range(4):
+                cols = slice(slot * P, (slot + 1) * P)
+                nc.tensor.transpose(bank[:, cols], by_parity[:, cols], ident[:])
+            grouped = stage.tile([P, 2 * P * 4], BF16, tag="grouped", bufs=6, align_bytes=64)
             dst = grouped[:].bitcast(F32).rearrange("p (j b e) -> p j b e", j=2, e=2)
             turned = bank[:].rearrange("p (j e b) -> p j b e", j=2, e=2)
             if on_vector:
@@ -171,18 +187,15 @@ def tile_leaky_recurrent_step_s1_kernel(
                 out=codes[(h, k_pass)][:].bitcast(FP8X4), scales=planes[(h, k_pass)][:], in_=grouped[:]
             )
 
-        steps = []
-        for h in range(2):
-            steps.extend((rates_sb[h], h, g, X_PASSES + g) for g in range(H_PASSES))
-            steps.extend((x_sb[h], h, g, g) for g in range(X_PASSES))
-        pending = None
-        for i, (src, h, g, k_pass) in enumerate(steps):
-            grouped = turn(src, h, g, i % 3 == 2)
-            if pending is not None:
-                quantize(*pending)
-            pending = (grouped, h, k_pass)
-        quantize(*pending)
-        spread_half(1)
+        def prepare(src, h, first_pass, count):
+            sorted_words = [sort_words(src, g) for g in range(count)]
+            pending = None
+            for g in range(count):
+                grouped = turn(sorted_words[g], on_vector=(g % 2 == 1))
+                if pending is not None:
+                    quantize(*pending)
+                pending = (grouped, h, first_pass + g)
+            quantize(*pending)
 
         tiles = [(h, j, a, c) for a in range(2) for h in range(2) for j in range(2) for c in range(2)]
         acc, base, u_new, r_new = {}, {}, {}, {}
@@ -190,7 +203,7 @@ def tile_leaky_recurrent_step_s1_kernel(
         def mx_pass(i, k_pass):
             h, j, a, c = tiles[i]
             if k_pass == 0:
-                acc[i] = next_bank()
+                acc[i] = take_bank(i if i < 4 else SUM_BANKS[(i - 4) % len(SUM_BANKS)])
             cols = slice(c * N_TILE, (c + 1) * N_TILE)
             if k_pass < X_PASSES:
                 rhs = weights[(k_pass, a)][:, c * N_TILE * 4 : (c + 1) * N_TILE * 4].bitcast(FP8X4)
@@ -211,7 +224,7 @@ def tile_leaky_recurrent_step_s1_kernel(
         def leak_times_u(i, engine):
             h, j, a, c = tiles[i]
             cols = slice(c * N_TILE, (c + 1) * N_TILE)
-            base[i] = stage.tile([P, N_TILE], F32, name="base%d" % i, tag="base", bufs=8)
+            base[i] = stage.tile([P, N_TILE], F32, name="base%d" % i, tag="base%d" % (1 if i == 4 else i), bufs=1)
             engine.tensor_tensor(out=base[i][:], in0=u_sb[(h, a)][:, j, cols], in1=leak_all[a][:, cols], op=MULT)
 
         def add_bias(i):
@@ -238,18 +251,48 @@ def tile_leaky_recurrent_step_s1_kernel(
                 nc.sync.dma_start(out=pair_rows(out_0, h)[:, j, half_cols], in_=u_new[(h, j, a)][:])
                 nc.sync.dma_start(out=pair_rows(out_1, h)[:, j, half_cols], in_=r_new[(h, j, a)][:])
 
-        first_wave = 4
-        for k_pass in range(4):
-            for i in range(first_wave):
-                mx_pass(i, k_pass)
-        for i in range(first_wave):
+        def passes(tile_numbers, k_passes):
+            for k_pass in k_passes:
+                for i in tile_numbers:
+                    mx_pass(i, k_pass)
+
+        wave = range(4)
+        spread_leak(0)
+        spread_bias(0)
+        prepare(x_sb[0], 0, 0, X_PASSES)
+        spread_leak(1)
+        passes(wave, range(X_PASSES))
+        prepare(rates_sb[0], 0, X_PASSES, H_PASSES)
+        passes(wave, range(X_PASSES, X_PASSES + 2))
+        sorted_x = [sort_words(x_sb[1], g) for g in range(X_PASSES)]
+        turned_x = [turn(words, on_vector=False) for words in sorted_x]
+        for i in wave:
+            passes([i], range(X_PASSES + 2, PASSES))
+        for i in (0, 1):
             leak_times_u(i, nc.vector)
-        for i in range(first_wave):
+        for i in (0, 1):
             add_bias(i)
-        for i in range(len(tiles)):
-            for k_pass in range(4 if i < first_wave else 0, PASSES):
-                mx_pass(i, k_pass)
-            if first_wave <= i + 1 < len(tiles):
+        sorted_words = [sort_words(rates_sb[1], g) for g in range(H_PASSES)]
+        for g in range(X_PASSES):
+            quantize(turned_x[g], 1, g)
+        turned = [turn(words, on_vector=False) for words in sorted_words]
+        finish(0)
+        for g in range(H_PASSES):
+            quantize(turned[g], 1, X_PASSES + g)
+        for i in (2, 3):
+            leak_times_u(i, nc.vector)
+        finish(1)
+        add_bias(2)
+        add_bias(3)
+        finish(2)
+        finish(3)
+        leak_times_u(4, nc.gpsimd)
+        add_bias(4)
+        for i in range(4, len(tiles)):
+            passes([i], range(PASSES))
+            if i == 5:
+                spread_bias(1)
+            if i + 1 < len(tiles):
                 leak_times_u(i + 1, nc.gpsimd)
                 add_bias(i + 1)
             finish(i)

from contextlib import ExitStack

import concourse.mybir as mybir
from concourse.masks import make_identity

B, D, H = 512, 1024, 2048
FLOPS = 2 * B * (D + H) * H

F32 = mybir.dt.float32
BF16 = mybir.dt.bfloat16
I32 = mybir.dt.int32
U32 = mybir.dt.uint32
U8 = mybir.dt.uint8
FP8X4 = mybir.dt.float8_e4m3fn_x4
FP4X4 = mybir.dt.float4_e2m1fn_x4
ADD = mybir.AluOpType.add
MULT = mybir.AluOpType.mult
TANH = mybir.ActivationFunctionType.Tanh

P = 128
N_TILE = 512
HALF = H // 2
X_PASSES = D // 512
H_PASSES = H // 512
PASSES = X_PASSES + H_PASSES
SUM_BANKS = (0, 5, 4, 1, 2, 3)
TURN_BANKS = (4, 5, 6)
BIAS_BANKS = (7, 6)


def tile_leaky_recurrent_step_s1_kernel(
    tc, x, rates, u, wx_words, wx_scales, wh_words, wh_scales, leak, bias, out_0, out_1
):
    nc = tc.nc
    with ExitStack() as ctx:
        keep = ctx.enter_context(tc.tile_pool(name="keep", bufs=1))
        stage = ctx.enter_context(tc.tile_pool(name="stage", bufs=4))
        psum = ctx.enter_context(tc.psum_pool(name="psum", bufs=1))
        ctx.enter_context(tc.manual_schedule())

        bank_uses = []

        def take_bank(number):
            bank_uses.append(number)
            return psum.tile([P, N_TILE], F32, name="bank_use%d" % len(bank_uses), tag="bank%d" % number)

        turn_uses = []

        def next_bank():
            turn_uses.append(0)
            return take_bank(TURN_BANKS[len(turn_uses) % len(TURN_BANKS)])

        def pair_rows(t, h):
            return t[256 * h : 256 * (h + 1), :].rearrange("(p j) n -> p j n", j=2)

        def load_pair(t, h, name):
            sb = keep.tile([P, 2 * t.shape[1]], BF16, name="%s%d" % (name, h), align_bytes=64)
            nc.sync.dma_start(out=sb[:], in_=pair_rows(t, h).rearrange("p j n -> p (j n)"))
            return sb

        vec_rows = keep.tile([P, 2 * P], BF16, align_bytes=64)
        nc.gpsimd.memset(vec_rows[:].bitcast(F32), 0.0)
        nc.sync.dma_start(out=vec_rows[0:8, :], in_=leak.rearrange("(r n) -> r n", r=8))
        nc.sync.dma_start(out=vec_rows[8:16, :], in_=bias.rearrange("(r n) -> r n", r=8))

        ident = keep.tile([P, P], F32, align_bytes=64)
        make_identity(nc, ident[:])

        wx_plane, wh_plane = {}, {}

        def clear_planes(a):
            wx_plane[a] = keep.tile([P, HALF], U8, name="wx_plane%d" % a, align_bytes=64)
            wh_plane[a] = keep.tile([P, H_PASSES, HALF], U8, name="wh_plane%d" % a, align_bytes=64)
            nc.vector.memset(wx_plane[a][:].bitcast(I32), 0)
            nc.vector.memset(wh_plane[a][:].bitcast(I32), 0)

        def load_wx_scales(a):
            cols = slice(a * HALF, (a + 1) * HALF)
            for q in range(4):
                nc.sync.dma_start(
                    out=wx_plane[a][32 * q + 4 : 32 * q + 12, :].bitcast(I32),
                    in_=wx_scales[:, 4 * q : 4 * q + 4, cols].bitcast(I32),
                )

        def load_wh_scales(a):
            cols = slice(a * HALF, (a + 1) * HALF)
            for r in range(4):
                nc.sync.dma_start(
                    out=wh_plane[a][r:P:32, :, :].bitcast(I32),
                    in_=wh_scales.rearrange("g q n -> q g n")[r:16:4, :, cols].bitcast(I32),
                )

        x_sb, rates_sb, u_sb = {}, {}, {}
        clear_planes(0)
        clear_planes(1)

        wx_rows = wx_words.rearrange("g p n t -> p g (n t)")
        wh_rows = wh_words.rearrange("g p n -> p g n")
        weights = {}

        def load_weights(rows, first_pass, g0, g1, a, col_bytes):
            width = HALF * col_bytes
            sb = keep.tile([P, g1 - g0, width], U8, name="w%d_%d" % (first_pass + g0, a), align_bytes=64)
            nc.sync.dma_start(
                out=sb[:].bitcast(I32), in_=rows[:, g0:g1, a * width : (a + 1) * width].bitcast(I32)
            )
            for g in range(g0, g1):
                weights[(first_pass + g, a)] = sb[:, g - g0, :]

        def load_u(h, a0, a1):
            sb = keep.tile([P, 2, (a1 - a0) * HALF], BF16, name="u%d_%d" % (h, a0), align_bytes=64)
            nc.sync.dma_start(out=sb[:], in_=pair_rows(u, h)[:, :, a0 * HALF : a1 * HALF])
            for a in range(a0, a1):
                u_sb[(h, a)] = sb[:, :, (a - a0) * HALF : (a - a0 + 1) * HALF]

        x_sb[0] = load_pair(x, 0, "x")
        load_wx_scales(0)
        load_weights(wx_rows, 0, 0, 1, 0, 4)
        load_weights(wx_rows, 0, 1, 2, 0, 4)
        rates_sb[0] = load_pair(rates, 0, "rates")
        load_wh_scales(0)
        load_weights(wh_rows, X_PASSES, 0, 2, 0, 2)
        load_weights(wh_rows, X_PASSES, 2, 4, 0, 2)
        x_sb[1] = load_pair(x, 1, "x")
        load_u(0, 0, 1)
        rates_sb[1] = load_pair(rates, 1, "rates")
        load_u(1, 0, 2)
        load_wx_scales(1)
        load_weights(wx_rows, 0, 0, 2, 1, 4)
        load_wh_scales(1)
        load_weights(wh_rows, X_PASSES, 0, 4, 1, 2)
        load_u(0, 1, 2)

        bank = next_bank()
        nc.tensor.transpose(bank[:, 0:P], vec_rows[:].bitcast(F32), ident[:])
        vec_cols = keep.tile([P, 16], F32, align_bytes=64)
        nc.scalar.copy(out=vec_cols[:], in_=bank[:, 0:16])

        def spread(bank, first_row):
            for j in range(4):
                row = first_row + j
                nc.tensor.transpose(
                    bank[:, j * P : (j + 1) * P], vec_cols[:, row : row + 1].to_broadcast([P, P]), ident[:]
                )

        leak_all, bias_bank = {}, {}

        def spread_leak(a):
            bank = next_bank()
            spread(bank, 4 * a)
            leak_all[a] = keep.tile([P, HALF], BF16, name="leak_all%d" % a, align_bytes=64)
            nc.scalar.copy(out=leak_all[a][:].bitcast(F32), in_=bank[:])

        def spread_bias(a):
            bias_bank[a] = take_bank(BIAS_BANKS[a])
            spread(bias_bank[a], 8 + 4 * a)

        codes, planes = {}, {}

        def sort_words(src, g):
            words = src[:].bitcast(F32).rearrange("p (j w) -> p j w", j=2)[:, :, 256 * g : 256 * (g + 1)]
            by_parity = stage.tile([P, 4 * P], F32, tag="by_parity", bufs=8, align_bytes=64)
            nc.vector.tensor_copy(
                out=by_parity[:].rearrange("p (j e c i) -> p j c e i", j=2, e=2, i=4),
                in_=words.rearrange("p j (c i e) -> p j c e i", e=2, i=4),
            )
            return by_parity

        def turn(by_parity, on_vector):
            bank = next_bank()
            for slot in range(4):
                cols = slice(slot * P, (slot + 1) * P)
                nc.tensor.transpose(bank[:, cols], by_parity[:, cols], ident[:])
            grouped = stage.tile([P, 2 * P * 4], BF16, tag="grouped", bufs=6, align_bytes=64)
            dst = grouped[:].bitcast(F32).rearrange("p (j b e) -> p j b e", j=2, e=2)
            turned = bank[:].rearrange("p (j e b) -> p j b e", j=2, e=2)
            if on_vector:
                nc.vector.tensor_copy(out=dst, in_=turned)
            else:
                nc.scalar.copy(out=dst, in_=turned)
            return grouped

        def quantize(grouped, h, k_pass):
            codes[(h, k_pass)] = keep.tile([P, 2 * P], U32, name="codes%d_%d" % (h, k_pass), align_bytes=64)
            planes[(h, k_pass)] = keep.tile([P, 2 * P], U8, name="plane%d_%d" % (h, k_pass), align_bytes=64)
            nc.vector.quantize_mx(
                out=codes[(h, k_pass)][:].bitcast(FP8X4), scales=planes[(h, k_pass)][:], in_=grouped[:]
            )

        def prepare(src, h, first_pass, count):
            sorted_words = [sort_words(src, g) for g in range(count)]
            pending = None
            for g in range(count):
                grouped = turn(sorted_words[g], on_vector=(g % 2 == 1))
                if pending is not None:
                    quantize(*pending)
                pending = (grouped, h, first_pass + g)
            quantize(*pending)

        tiles = [(h, j, a, c) for a in range(2) for h in range(2) for j in range(2) for c in range(2)]
        acc, base, u_new, r_new = {}, {}, {}, {}

        def mx_pass(i, k_pass):
            h, j, a, c = tiles[i]
            if k_pass == 0:
                acc[i] = take_bank(i if i < 4 else SUM_BANKS[(i - 4) % len(SUM_BANKS)])
            cols = slice(c * N_TILE, (c + 1) * N_TILE)
            if k_pass < X_PASSES:
                rhs = weights[(k_pass, a)][:, c * N_TILE * 4 : (c + 1) * N_TILE * 4].bitcast(FP8X4)
                rhs_scale = wx_plane[a][4 * (k_pass + 1) : P, cols]
            else:
                rhs = weights[(k_pass, a)][:, c * N_TILE * 2 : (c + 1) * N_TILE * 2].bitcast(FP4X4)
                rhs_scale = wh_plane[a][:, k_pass - X_PASSES, cols]
            nc.tensor.matmul_mx(
                out=acc[i][:],
                lhsT=codes[(h, k_pass)][:, j * P : (j + 1) * P].bitcast(FP8X4),
                lhsT_scale=planes[(h, k_pass)][:, j * P : (j + 1) * P],
                rhs=rhs,
                rhs_scale=rhs_scale,
                start=(k_pass == 0),
                stop=(k_pass == PASSES - 1),
            )

        def leak_times_u(i, engine):
            h, j, a, c = tiles[i]
            cols = slice(c * N_TILE, (c + 1) * N_TILE)
            base[i] = stage.tile([P, N_TILE], F32, name="base%d" % i, tag="base%d" % (1 if i == 4 else i), bufs=1)
            engine.tensor_tensor(out=base[i][:], in0=u_sb[(h, a)][:, j, cols], in1=leak_all[a][:, cols], op=MULT)

        def add_bias(i):
            h, j, a, c = tiles[i]
            cols = slice(c * N_TILE, (c + 1) * N_TILE)
            nc.vector.tensor_tensor(
                out=base[i][:], in0=base[i][:], in1=bias_bank[a][:].bitcast(BF16)[:, cols], op=ADD
            )

        def finish(i):
            h, j, a, c = tiles[i]
            if c == 0:
                u_new[(h, j, a)] = keep.tile([P, HALF], F32, name="u_new%d" % i)
                r_new[(h, j, a)] = keep.tile([P, HALF], F32, name="r_new%d" % i)
            cols = slice(c * N_TILE, (c + 1) * N_TILE)
            nc.vector.tensor_tensor(out=u_new[(h, j, a)][:, cols], in0=base[i][:], in1=acc[i][:], op=ADD)
            nc.scalar.activation(out=r_new[(h, j, a)][:, cols], in_=u_new[(h, j, a)][:, cols], func=TANH)
            if i >= len(tiles) - 2:
                out_cols = slice(a * HALF + c * N_TILE, a * HALF + (c + 1) * N_TILE)
                nc.sync.dma_start(out=pair_rows(out_0, h)[:, j, out_cols], in_=u_new[(h, j, a)][:, cols])
                nc.sync.dma_start(out=pair_rows(out_1, h)[:, j, out_cols], in_=r_new[(h, j, a)][:, cols])
            elif c == 1:
                half_cols = slice(a * HALF, (a + 1) * HALF)
                nc.sync.dma_start(out=pair_rows(out_0, h)[:, j, half_cols], in_=u_new[(h, j, a)][:])
                nc.sync.dma_start(out=pair_rows(out_1, h)[:, j, half_cols], in_=r_new[(h, j, a)][:])

        def passes(tile_numbers, k_passes):
            for k_pass in k_passes:
                for i in tile_numbers:
                    mx_pass(i, k_pass)

        wave = range(4)
        spread_leak(0)
        spread_bias(0)
        prepare(x_sb[0], 0, 0, X_PASSES)
        spread_leak(1)
        passes(wave, range(X_PASSES))
        prepare(rates_sb[0], 0, X_PASSES, H_PASSES)
        passes(wave, range(X_PASSES, X_PASSES + 2))
        sorted_x = [sort_words(x_sb[1], g) for g in range(X_PASSES)]
        turned_x = [turn(words, on_vector=False) for words in sorted_x]
        for i in wave:
            passes([i], range(X_PASSES + 2, PASSES))
        for i in (0, 1):
            leak_times_u(i, nc.vector)
        for i in (0, 1):
            add_bias(i)
        sorted_words = [sort_words(rates_sb[1], g) for g in range(H_PASSES)]
        for g in range(X_PASSES):
            quantize(turned_x[g], 1, g)
        turned = [turn(words, on_vector=False) for words in sorted_words]
        finish(0)
        for g in range(H_PASSES):
            quantize(turned[g], 1, X_PASSES + g)
        for i in (2, 3):
            leak_times_u(i, nc.vector)
        finish(1)
        add_bias(2)
        add_bias(3)
        finish(2)
        finish(3)
        leak_times_u(4, nc.gpsimd)
        add_bias(4)
        for i in range(4, len(tiles)):
            passes([i], range(PASSES))
            if i == 5:
                spread_bias(1)
            if i + 1 < len(tiles):
                leak_times_u(i + 1, nc.gpsimd)
                add_bias(i + 1)
            finish(i)
